import numpy as np
import ml_dtypes


def mxq(x, axis, fmt="e4m3"):
    dtype, down = {"e4m3": (ml_dtypes.float8_e4m3fn, 7), "e5m2": (ml_dtypes.float8_e5m2, 14)}[fmt]
    v = np.moveaxis(np.asarray(x, np.float32).astype(ml_dtypes.bfloat16).astype(np.float64), axis, -1)
    blocks = v.reshape(v.shape[:-1] + (-1, 32))
    amax = np.abs(blocks).max(-1, keepdims=True)
    byte = np.maximum(np.where(amax > 0, np.frexp(amax)[1] - 1 + 127, 0) - down, 1)
    scale = np.exp2(byte - 127.0)
    codes = (blocks / scale).astype(np.float32).astype(dtype).astype(np.float64)
    return np.moveaxis((codes * scale).reshape(v.shape), -1, axis)


WIDE = False


def mx_kscale(k):
    if not WIDE:
        return np.ones(k)
    levels = np.array([10, -10, 5, -5, 0])
    if k % 512:
        return np.exp2(np.random.permutation(np.resize(levels, k // 32))).repeat(32)
    a = np.empty((k // 512, 16))
    for p in range(k // 512):
        a[p, :8] = np.random.permutation(np.resize(levels, 8))
        for g in range(8):
            far = levels[np.abs(levels - a[p, g]) >= 10]
            a[p, g + 8] = far[np.random.randint(len(far))]
    return np.exp2(a.ravel()).repeat(32)


def f64(x):
    return np.asarray(x).astype(np.float64)


def striped(idx):
    return np.tile(idx.reshape(-1, 16).T, (8, 1)).astype(np.uint16)


def unstriped(offs):
    return offs[:16].T.reshape(-1).astype(np.int64)


E2M1 = np.array([0.0, 0.5, 1.0, 1.5, 2.0, 3.0, 4.0, 6.0, -0.0, -0.5, -1.0, -1.5, -2.0, -3.0, -4.0, -6.0])


def pack_weight(w, fmt):
    k, n = w.shape
    w = f64(np.asarray(w, np.float32).astype(ml_dtypes.bfloat16)).reshape(k // 32, 32, n)
    amax = np.abs(w).max(1)
    if fmt == "e4m3":
        byte = np.frexp(amax)[1] - 1 + 127 - 7
    else:
        mant, ex = np.frexp(amax / 6.0)
        byte = np.where(mant > 0.5, ex, ex - 1) + 127
    byte = np.clip(np.where(amax > 0, byte, 1), 1, 254)
    scaled = (w * np.exp2(127.0 - byte)[:, None, :]).reshape(k, n).astype(np.float32)
    by_word = np.ascontiguousarray(scaled.reshape(k // 512, 128, 4, n).transpose(0, 1, 3, 2))
    if fmt == "e4m3":
        words = by_word.astype(ml_dtypes.float8_e4m3fn).view(np.uint8)
    else:
        c = by_word.astype(ml_dtypes.float4_e2m1fn).view(np.uint8) & 0xF
        words = (c[..., 0::2] | (c[..., 1::2] << 4)).reshape(k // 512, 128, 2 * n)
    return np.ascontiguousarray(words), np.ascontiguousarray(byte.astype(np.uint8).reshape(k // 512, 16, n))


def unpack_weight(words, scales, fmt):
    g, _, n = scales.shape
    words = np.ascontiguousarray(words).reshape(g, 128, n, -1)
    if fmt == "e4m3":
        vals = words.view(ml_dtypes.float8_e4m3fn).astype(np.float64)
    else:
        nib = np.empty((g, 128, n, 4), np.uint8)
        nib[..., 0::2] = words & 0xF
        nib[..., 1::2] = words >> 4
        vals = E2M1[nib]
    vals = vals * np.repeat(np.exp2(scales.astype(np.float64) - 127.0), 8, axis=1)[..., None]
    return vals.transpose(0, 1, 3, 2).reshape(g * 512, n)


def planes(y):
    n, m = y.shape
    v = y.astype(np.float32).astype(ml_dtypes.bfloat16).astype(np.float64).reshape(n // 32, 32, m)
    top = np.abs(v).max(1)
    byte = np.clip(np.where(top > 0, np.frexp(top)[1] - 1 + 127 - 7, 1), 1, 254)
    codes = (v * np.exp2(127.0 - byte)[:, None, :]).reshape(n, m).astype(np.float32).astype(ml_dtypes.float8_e4m3fn).view(np.uint8)
    words = codes.reshape(n // 512, 128, 4, m).transpose(0, 1, 3, 2)
    return np.ascontiguousarray(words), np.ascontiguousarray(byte.astype(np.uint8).reshape(n // 512, 16, m))


def relu2(v):
    return np.maximum(v, 0.0) ** 2


K, T, E1, C1, E2, C2, H = 1536, 768, 6, 128, 3, 256, 512
N = 512


def deal(E, C):
    slot_token = np.random.permutation(T)
    return slot_token, None, np.random.uniform(0.2, 1.0, T)


def by_expert(wq, xq, E, C):
    return np.concatenate([wq[e].T @ xq[:, e * C:(e + 1) * C] for e in range(E)], axis=1)


def setup_inputs():
    n = np.random.standard_normal
    s = mx_kscale(K)
    u = mx_kscale(H)
    slots1, pos1, g1 = deal(E1, C1)
    slots2, pos2, g2 = deal(E2, C2)
    x = pack_weight(n((K, T)) * s[:, None], "e4m3")
    w1 = [pack_weight(m, "e4m3") for m in n((E1, K, H)) / np.sqrt(K) / s[None, :, None] * u]
    w2 = [pack_weight(m, "e2m1") for m in n((E2, H, N)) / np.sqrt(H) / u[None, :, None] ** 2]
    return {
        "x_words": x[0],
        "x_scales": x[1],
        "w1_words": np.stack([m[0] for m in w1]),
        "w1_scales": np.stack([m[1] for m in w1]),
        "w2_words": np.stack([m[0] for m in w2]),
        "w2_scales": np.stack([m[1] for m in w2]),
        "gate1": (np.tile(g1, (128, 1))).astype(np.float32),
        "gate2": (np.tile(g2, (128, 1))).astype(np.float32),
        "offs": striped(slots1),
        "offs2": striped(slots2),
    }


def reference(x_words, x_scales, w1_words, w1_scales, w2_words, w2_scales, gate1, gate2, offs, offs2):
    w1 = np.stack([unpack_weight(w1_words[e], w1_scales[e], "e4m3") for e in range(E1)])
    w2 = np.stack([unpack_weight(w2_words[e], w2_scales[e], "e2m1") for e in range(E2)])
    idx, idx2 = unstriped(offs), unstriped(offs2)
    xq = unpack_weight(x_words, x_scales, "e4m3")[:, idx]
    h = relu2(by_expert(w1, xq, E1, C1))
    c = np.zeros((H, T))
    c[:, idx] = f64(gate1[:1]) * h
    y = by_expert(w2, mxq(c[:, idx2], 0, "e4m3"), E2, C2)
    out = np.zeros((N, T))
    out[:, idx2] = f64(gate2[:1]) * y
    out_0 = out
    return (out_0,) + planes(out_0)

@@ -1,0 +1,244 @@
+from contextlib import ExitStack
+
+import concourse.mybir as mybir
+from concourse.masks import make_identity
+
+K, T, E1, C1, E2, C2, H, N = 1536, 768, 6, 128, 3, 256, 512, 512
+FLOPS = 2 * T * (K * H + H * N)
+
+F32 = mybir.dt.float32
+BF16 = mybir.dt.bfloat16
+I32 = mybir.dt.int32
+U32 = mybir.dt.uint32
+U16 = mybir.dt.uint16
+U8 = mybir.dt.uint8
+FP8X4 = mybir.dt.float8_e4m3fn_x4
+FP4X4 = mybir.dt.float4_e2m1fn_x4
+ACT = mybir.ActivationFunctionType
+MULT = mybir.AluOpType.mult
+
+P = 128
+PASSES = K // 512
+HALF = T // 2
+EH = E1 // 2
+VECTOR_GATED = (1, 3)
+SPLIT = 512
+
+
+def tile_moe_ser_relu2_kernel(
+    tc, x_words, x_scales, w1_words, w1_scales, w2_words, w2_scales, gate1, gate2, offs, offs2, out_0, out_1, out_2
+):
+    nc = tc.nc
+    with ExitStack() as ctx:
+        keep = ctx.enter_context(tc.tile_pool(name="keep", bufs=1))
+        ring = ctx.enter_context(tc.tile_pool(name="ring", bufs=3))
+        psum = ctx.enter_context(tc.psum_pool(name="psum", bufs=1))
+
+        list1 = keep.tile([P, T // 16], U16, name="list1")
+        list2 = keep.tile([P, T // 16], U16, name="list2")
+        xw = keep.tile([P, PASSES * T], I32, name="xw", align_bytes=64)
+        xs = keep.tile([P, T], U8, name="xs", align_bytes=64)
+        w1w = [keep.tile([P, PASSES, H], I32, name=f"w1w{e}", align_bytes=64) for e in range(E1)]
+        w1s = [keep.tile([P, EH * PASSES, H], U8, name=f"w1s{h}", align_bytes=64) for h in range(2)]
+        w2raw = keep.tile([P, E2, 2 * N], U8, name="w2raw", align_bytes=64)
+        w2sraw = keep.tile([P, N], U8, name="w2sraw", align_bytes=64)
+        w2sdealt = keep.tile([P, N], U8, name="w2sdealt", align_bytes=64)
+        w2w = [keep.tile([P, 2 * N], U8, name=f"w2w{f}", tag=f"w2w{f}", align_bytes=64) for f in range(E2)]
+        w2s = keep.tile([P, E2, N], U8, name="w2s", align_bytes=64)
+        g1rows = keep.tile([P, P], F32, name="g1rows")
+        g1 = keep.tile([P, E1], F32, name="g1")
+        g2 = keep.tile([P, T], F32, name="g2", tag="g2", align_bytes=64)
+        ident = keep.tile([P, P], F32, name="ident")
+
+        nc.gpsimd.memset(xs[:].bitcast(I32), 0)
+        nc.vector.memset(w1s[0][:].rearrange("p a i -> p (a i)").bitcast(I32), 0)
+        nc.vector.memset(w1s[1][:].rearrange("p a i -> p (a i)").bitcast(I32), 0)
+        nc.gpsimd.memset(g1rows[:], 0.0)
+        nc.gpsimd.memset(w2sraw[:].bitcast(I32), 0)
+        nc.vector.memset(w2s[:].rearrange("p f n -> p (f n)").bitcast(I32), 0)
+
+        def load_x(s):
+            nc.sync.dma_start(out=xw[:, s * T : (s + 1) * T], in_=x_words[s].rearrange("p t d -> p (t d)").bitcast(I32))
+
+        def load_w1(e):
+            nc.sync.dma_start(out=w1w[e][:], in_=w1_words[e].rearrange("s p i d -> p s (i d)").bitcast(I32))
+
+        def load_w1_scales(h):
+            rows = w1_scales.rearrange("e s b i -> b (e s) i")
+            for q in range(4):
+                first = 32 * q + 4 * h
+                nc.gpsimd.dma_start(
+                    out=w1s[h][first : first + 4, :, :].bitcast(I32),
+                    in_=rows[4 * q : 4 * q + 4, EH * PASSES * h : EH * PASSES * (h + 1), :].bitcast(I32),
+                )
+
+        nc.sync.dma_start(list1[:], offs)
+        load_x(0)
+        for q in range(4):
+            nc.scalar.dma_start(
+                out=xs[32 * q : 32 * q + 4 * PASSES, :].bitcast(I32), in_=x_scales[:, 4 * q : 4 * q + 4, :].bitcast(I32)
+            )
+        load_x(1)
+        load_x(2)
+        load_w1(0)
+        load_w1_scales(0)
+        make_identity(nc, ident[:])
+        nc.scalar.dma_start(out=g1rows[0:E1, :], in_=gate1[0:1, :].rearrange("o (e p) -> (o e) p", p=P))
+        nc.sync.dma_start(out=w2raw[:].bitcast(I32), in_=w2_words.rearrange("f s p b -> p (f s) b").bitcast(I32))
+        load_w1(1)
+        nc.scalar.dma_start(
+            out=w2sraw[0 : 16 * E2, :].bitcast(I32), in_=w2_scales.rearrange("f s b n -> b (f s) n").bitcast(I32)
+        )
+        load_w1(2)
+        load_w1_scales(1)
+        for e in range(EH, E1):
+            load_w1(e)
+        nc.sync.dma_start(list2[:], offs2)
+        nc.sync.dma_start(out=g2[:], in_=gate2)
+
+        xg = [[keep.tile([P, HALF], U32, name=f"xg{h}_{s}", align_bytes=64) for s in range(PASSES)] for h in range(2)]
+        xsg = [keep.tile([P, HALF], U8, name=f"xsg{h}", align_bytes=64) for h in range(2)]
+        for h in range(2):
+            part = list1[:, h * HALF // 16 : (h + 1) * HALF // 16]
+            for s in range(PASSES):
+                window = xw[:, s * T : (s + 1) * T] if h == 0 else xw[:, s * T :]
+                nc.vector.tensor_copy(xg[h][s][:], window.bitcast(U32).indirect(part))
+            nc.vector.tensor_copy(xsg[h][:], xs[:].indirect(part))
+
+        nc.vector.tensor_copy(
+            out=w2sdealt[:].rearrange("p (t m) -> p t m", t=4), in_=w2sraw[:].rearrange("p (m t) -> p t m", t=4)
+        )
+        for q in range(4):
+            nc.sync.dma_start(
+                out=w2s[32 * q : 32 * q + 4, :, :].bitcast(I32),
+                in_=w2sdealt[4 * E2 * q : 4 * E2 * (q + 1), :].bitcast(I32),
+            )
+
+        g1ps = psum.tile([P, N], F32, name="g1ps", tag="second", bufs=4)
+        nc.tensor.transpose(g1ps[:, 0:P], g1rows[:], ident[:])
+        nc.scalar.activation(out=g1[:], in_=g1ps[:, 0:E1], func=ACT.Copy)
+        for f in range(E2):
+            nc.scalar.copy(
+                out=w2w[f][:].bitcast(U16).rearrange("p (t m) -> p t m", t=4),
+                in_=w2raw[:, f, :].bitcast(U16).rearrange("p (m t) -> p t m", t=4),
+            )
+
+        cpair = [keep.tile([P, T], F32, name=f"cpair{u}") for u in range(2)]
+        for e in range(E1):
+            h, j = divmod(e, EH)
+            cols = slice(j * C1, (j + 1) * C1)
+            acc = psum.tile([P, H], F32, name="acc", tag="first", bufs=2)
+            for s in range(PASSES):
+                nc.tensor.matmul_mx(
+                    out=acc[:],
+                    lhsT=xg[h][s][:, cols].bitcast(FP8X4),
+                    lhsT_scale=xsg[h][4 * s : P, cols],
+                    rhs=w1w[e][:, s, :].bitcast(FP8X4),
+                    rhs_scale=w1s[h][4 * h : P, j * PASSES + s, :],
+                    start=(s == 0),
+                    stop=(s == PASSES - 1),
+                )
+            r = ring.tile([P, H], F32, name="r")
+            nc.scalar.activation(
+                out=r[:].rearrange("m (u p j) -> m u p j", u=2, j=2),
+                in_=acc[:].rearrange("m (p u j) -> m u p j", u=2, j=2),
+                func=ACT.Relu,
+            )
+            hb = ring.tile([P, H], BF16, name="hb")
+            if e not in VECTOR_GATED:
+                r2 = ring.tile([P, H], F32, name="r2")
+                nc.scalar.activation(out=r2[:], in_=r[:], func=ACT.Square)
+                nc.scalar.activation(out=hb[:], in_=r2[:], func=ACT.Copy, scale=g1[:, e : e + 1])
+            else:
+                nc.vector.scalar_tensor_tensor(
+                    out=hb[:], in0=r[:], scalar=g1[:, e : e + 1], in1=r[:], op0=MULT, op1=MULT
+                )
+            turned = psum.tile([P, 2, P], F32, name="turned", tag="turn", bufs=2)
+            pairs = hb[:].bitcast(F32)
+            for u in range(2):
+                nc.tensor.transpose(turned[:, u, :], pairs[:, u * P : (u + 1) * P], ident[:])
+            ct = ring.tile([P, 2, P], F32, name="ct")
+            nc.scalar.copy(out=ct[:], in_=turned[:])
+            part = list1[:, e * C1 // 16 : (e + 1) * C1 // 16]
+            for u in range(2):
+                nc.vector.tensor_copy(cpair[u][:].indirect(part), ct[:, u, :])
+
+        gated = {}
+        for f in range(E2):
+            part = list2[:, f * C2 // 16 : (f + 1) * C2 // 16]
+            gp = ring.tile([P, 2, C2], U32, name="gp")
+            for u in range(2):
+                nc.vector.tensor_copy(gp[:, u, :], cpair[u][:].bitcast(U32).indirect(part))
+            cb = ring.tile([P, 4 * C2], BF16, name="cb", align_bytes=64)
+            nc.scalar.copy(
+                out=cb[:].bitcast(U32).rearrange("p (m u) -> p m u", u=2), in_=gp[:].rearrange("p u m -> p m u")
+            )
+            cq = ring.tile([P, C2], U32, name="cq", align_bytes=64)
+            cs = ring.tile([P, C2], U8, name="cs", align_bytes=64)
+            nc.vector.quantize_mx(out=cq[:].bitcast(FP8X4), scales=cs[:], in_=cb[:])
+            for a in range(2):
+                acc = psum.tile([P, N], F32, name="acc2", tag="second", bufs=4)
+                for j in range(2):
+                    t = 2 * a + j
+                    nc.tensor.matmul_mx(
+                        out=acc[:, j * C2 : (j + 1) * C2],
+                        lhsT=w2w[f][:, 2 * t * P : 2 * (t + 1) * P].bitcast(FP4X4),
+                        lhsT_scale=w2s[:, f, t * P : (t + 1) * P],
+                        rhs=cq[:].bitcast(FP8X4),
+                        rhs_scale=cs[:],
+                        start=True,
+                        stop=True,
+                    )
+                yg = keep.tile([P, 2, C2], F32, name=f"yg{f}_{a}")
+                nc.vector.tensor_tensor(
+                    out=yg[:],
+                    in0=acc[:].rearrange("p (j m) -> p j m", j=2),
+                    in1=g2[:, f * C2 : (f + 1) * C2].unsqueeze(1).to_broadcast([P, 2, C2]),
+                    op=MULT,
+                )
+                for j in range(2):
+                    gated[(f, 2 * a + j)] = yg[:, j, :]
+
+        tags = ("plane0", "w2w2", "plane2", "g2")
+        plane = [keep.tile([P, T], F32, name=f"plane{t}", tag=tags[t], align_bytes=64) for t in range(4)]
+
+        def scatter(f, t, on_scalar):
+            window = plane[t][:].indirect(list2[:, f * C2 // 16 : (f + 1) * C2 // 16])
+            if on_scalar:
+                nc.scalar.activation(out=window, in_=gated[(f, t)], func=ACT.Copy)
+            else:
+                nc.vector.tensor_copy(window, gated[(f, t)])
+
+        rows = out_0.rearrange("(p t) n -> p t n", t=4)
+        comb = keep.tile([P, 4, T], F32, name="comb")
+        for f, t in ((0, 0), (0, 2), (1, 0), (2, 0), (0, 1), (1, 1), (2, 1)):
+            scatter(f, t, True)
+        for f, t in ((1, 2), (2, 2), (0, 3), (1, 3), (2, 3)):
+            scatter(f, t, False)
+        for t in (2, 0):
+            nc.sync.dma_start(out=comb[:, t, :], in_=plane[t][:])
+            nc.sync.dma_start(out=rows[:, t, :], in_=plane[t][:])
+        nc.scalar.dma_start(out=rows[:, 1, :], in_=plane[1][:])
+        nc.sync.dma_start(out=rows[:, 3, :], in_=plane[3][:])
+        nc.vector.tensor_copy(out=comb[:, 3, :], in_=plane[3][:])
+        nc.vector.tensor_copy(out=comb[:, 1, :SPLIT], in_=plane[1][:, :SPLIT])
+        nc.scalar.copy(out=comb[:, 1, SPLIT:], in_=plane[1][:, SPLIT:])
+
+        codes = keep.tile([P, T], I32, name="codes", align_bytes=64)
+        scales = keep.tile([P, T], U8, name="scales", align_bytes=64)
+        words_out = out_1[0].rearrange("p t d -> p (t d)").bitcast(I32)
+        for cols in (slice(0, SPLIT), slice(SPLIT, T)):
+            ob = keep.tile([P, 4 * (cols.stop - cols.start)], BF16, name=f"ob{cols.start}", align_bytes=64)
+            dst = ob[:].rearrange("p (c i t) -> p c t i", i=4, t=4)
+            src = comb[:, :, cols].rearrange("p t (c i) -> p c t i", i=4)
+            if cols.start:
+                nc.scalar.copy(out=dst, in_=src)
+            else:
+                nc.vector.tensor_copy(out=dst, in_=src)
+            nc.vector.quantize_mx(out=codes[:, cols].bitcast(FP8X4), scales=scales[:, cols], in_=ob[:])
+            nc.sync.dma_start(out=words_out[:, cols], in_=codes[:, cols])
+        for q in range(4):
+            queue = nc.scalar if q % 2 else nc.sync
+            queue.dma_start(
+                out=out_2[0, 4 * q : 4 * q + 4, :].bitcast(I32), in_=scales[32 * q : 32 * q + 4, :].bitcast(I32)
+            )

@@ -19,10 +19,11 @@ MULT = mybir.AluOpType.mult
 
 P = 128
 PASSES = K // 512
-HALF = T // 2
+EARLY = 3
+SCALAR_GATED = 4
+WIDE = 1024
 EH = E1 // 2
-VECTOR_GATED = (1, 3)
-SPLIT = 512
+TOK = 256
 
 
 def tile_moe_ser_relu2_kernel(
@@ -37,13 +38,12 @@ def tile_moe_ser_relu2_kernel(
         list1 = keep.tile([P, T // 16], U16, name="list1")
         list2 = keep.tile([P, T // 16], U16, name="list2")
         xw = keep.tile([P, PASSES * T], I32, name="xw", align_bytes=64)
-        xs = keep.tile([P, T], U8, name="xs", align_bytes=64)
+        xs = keep.tile([P, T], U8, name="xs", tag="xs", align_bytes=64)
+        xs_late = keep.tile([P, T], U8, name="xs_late", tag="xs_late", align_bytes=64)
         w1w = [keep.tile([P, PASSES, H], I32, name=f"w1w{e}", align_bytes=64) for e in range(E1)]
         w1s = [keep.tile([P, EH * PASSES, H], U8, name=f"w1s{h}", align_bytes=64) for h in range(2)]
         w2raw = keep.tile([P, E2, 2 * N], U8, name="w2raw", align_bytes=64)
         w2sraw = keep.tile([P, N], U8, name="w2sraw", align_bytes=64)
-        w2sdealt = keep.tile([P, N], U8, name="w2sdealt", align_bytes=64)
-        w2w = [keep.tile([P, 2 * N], U8, name=f"w2w{f}", tag=f"w2w{f}", align_bytes=64) for f in range(E2)]
         w2s = keep.tile([P, E2, N], U8, name="w2s", align_bytes=64)
         g1rows = keep.tile([P, P], F32, name="g1rows")
         g1 = keep.tile([P, E1], F32, name="g1")
@@ -51,88 +51,107 @@ def tile_moe_ser_relu2_kernel(
         ident = keep.tile([P, P], F32, name="ident")
 
         nc.gpsimd.memset(xs[:].bitcast(I32), 0)
-        nc.vector.memset(w1s[0][:].rearrange("p a i -> p (a i)").bitcast(I32), 0)
-        nc.vector.memset(w1s[1][:].rearrange("p a i -> p (a i)").bitcast(I32), 0)
         nc.gpsimd.memset(g1rows[:], 0.0)
         nc.gpsimd.memset(w2sraw[:].bitcast(I32), 0)
-        nc.vector.memset(w2s[:].rearrange("p f n -> p (f n)").bitcast(I32), 0)
+        make_identity(nc, ident[:])
 
-        def load_x(s):
-            nc.sync.dma_start(out=xw[:, s * T : (s + 1) * T], in_=x_words[s].rearrange("p t d -> p (t d)").bitcast(I32))
+        def load_x(first, last):
+            nc.sync.dma_start(
+                out=xw[:, first * T : last * T].rearrange("p (s t) -> p s t", t=T),
+                in_=x_words[first:last].rearrange("s p t d -> p s (t d)").bitcast(I32),
+            )
 
         def load_w1(e):
             nc.sync.dma_start(out=w1w[e][:], in_=w1_words[e].rearrange("s p i d -> p s (i d)").bitcast(I32))
 
-        def load_w1_scales(h):
+        def load_w1_scales(h, r):
             rows = w1_scales.rearrange("e s b i -> b (e s) i")
-            for q in range(4):
-                first = 32 * q + 4 * h
-                nc.gpsimd.dma_start(
-                    out=w1s[h][first : first + 4, :, :].bitcast(I32),
-                    in_=rows[4 * q : 4 * q + 4, EH * PASSES * h : EH * PASSES * (h + 1), :].bitcast(I32),
-                )
+            nc.sync.dma_start(
+                out=w1s[h][4 * h + r : P : 32, :, :].bitcast(I32),
+                in_=rows[r:16:4, EH * PASSES * h : EH * PASSES * (h + 1), :].bitcast(I32),
+            )
 
         nc.sync.dma_start(list1[:], offs)
-        load_x(0)
+        load_x(0, 1)
+        for r in range(3):
+            load_w1_scales(0, r)
+        load_x(1, PASSES)
+        load_w1(0)
+        load_w1_scales(0, 3)
         for q in range(4):
-            nc.scalar.dma_start(
+            nc.sync.dma_start(
                 out=xs[32 * q : 32 * q + 4 * PASSES, :].bitcast(I32), in_=x_scales[:, 4 * q : 4 * q + 4, :].bitcast(I32)
             )
-        load_x(1)
-        load_x(2)
-        load_w1(0)
-        load_w1_scales(0)
-        make_identity(nc, ident[:])
-        nc.scalar.dma_start(out=g1rows[0:E1, :], in_=gate1[0:1, :].rearrange("o (e p) -> (o e) p", p=P))
-        nc.sync.dma_start(out=w2raw[:].bitcast(I32), in_=w2_words.rearrange("f s p b -> p (f s) b").bitcast(I32))
+        nc.sync.dma_start(out=g1rows[0:E1, :], in_=gate1[0:1, :].rearrange("o (e p) -> (o e) p", p=P))
         load_w1(1)
-        nc.scalar.dma_start(
+        nc.sync.dma_start(out=w2raw[:].bitcast(I32), in_=w2_words.rearrange("f s p b -> p (f s) b").bitcast(I32))
+        nc.sync.dma_start(
             out=w2sraw[0 : 16 * E2, :].bitcast(I32), in_=w2_scales.rearrange("f s b n -> b (f s) n").bitcast(I32)
         )
         load_w1(2)
-        load_w1_scales(1)
+        for r in range(4):
+            load_w1_scales(1, r)
         for e in range(EH, E1):
             load_w1(e)
         nc.sync.dma_start(list2[:], offs2)
         nc.sync.dma_start(out=g2[:], in_=gate2)
 
-        xg = [[keep.tile([P, HALF], U32, name=f"xg{h}_{s}", align_bytes=64) for s in range(PASSES)] for h in range(2)]
-        xsg = [keep.tile([P, HALF], U8, name=f"xsg{h}", align_bytes=64) for h in range(2)]
-        for h in range(2):
-            part = list1[:, h * HALF // 16 : (h + 1) * HALF // 16]
-            for s in range(PASSES):
-                window = xw[:, s * T : (s + 1) * T] if h == 0 else xw[:, s * T :]
-                nc.vector.tensor_copy(xg[h][s][:], window.bitcast(U32).indirect(part))
-            nc.vector.tensor_copy(xsg[h][:], xs[:].indirect(part))
+        cut = EARLY * C1
+        early, late = list1[:, : cut // 16], list1[:, cut // 16 :]
+        xg_early = keep.tile([P, PASSES, cut], U32, name="xg_early", align_bytes=64)
+        xg_first = keep.tile([P, T - cut], U32, name="xg_first", align_bytes=64)
+        xsg_early = keep.tile([P, cut], U8, name="xsg_early", align_bytes=64)
+        xsg_late = keep.tile([P, T - cut], U8, name="xsg_late", align_bytes=64)
 
+        def window(s):
+            return xw[:, s * T : (s + 1) * T].bitcast(U32)
+
+        for s in range(PASSES):
+            nc.vector.tensor_copy(xg_early[:, s, :], window(s).indirect(early))
+        nc.vector.tensor_copy(xsg_early[:], xs[:].indirect(early))
+        nc.vector.tensor_copy(xg_first[:], window(0).indirect(late))
+        nc.vector.tensor_copy(out=xs_late[:].bitcast(I32), in_=xs[:].bitcast(I32))
+        xg_rest = keep.tile([P, PASSES - 1, T - cut], U32, name="xg_rest", tag="xs", align_bytes=64)
+        for s in range(1, PASSES):
+            nc.vector.tensor_copy(xg_rest[:, s - 1, :], window(s).indirect(late))
+        nc.vector.tensor_copy(xsg_late[:], xs_late[:].indirect(late))
+
+        def tokens(e, s):
+            if e < EARLY:
+                cols = slice(e * C1, (e + 1) * C1)
+                return xg_early[:, s, cols], xsg_early[4 * s : P, cols]
+            cols = slice((e - EARLY) * C1, (e - EARLY + 1) * C1)
+            words = xg_first[:, cols] if s == 0 else xg_rest[:, s - 1, cols]
+            return words, xsg_late[4 * s : P, cols]
+
+        w2sdealt = keep.tile([P, N], U8, name="w2sdealt", tag="xs_late", align_bytes=64)
         nc.vector.tensor_copy(
             out=w2sdealt[:].rearrange("p (t m) -> p t m", t=4), in_=w2sraw[:].rearrange("p (m t) -> p t m", t=4)
         )
         for q in range(4):
-            nc.sync.dma_start(
+            nc.gpsimd.dma_start(
                 out=w2s[32 * q : 32 * q + 4, :, :].bitcast(I32),
                 in_=w2sdealt[4 * E2 * q : 4 * E2 * (q + 1), :].bitcast(I32),
             )
 
-        g1ps = psum.tile([P, N], F32, name="g1ps", tag="second", bufs=4)
+        g1ps = psum.tile([P, N], F32, name="g1ps", tag="second", bufs=5)
         nc.tensor.transpose(g1ps[:, 0:P], g1rows[:], ident[:])
         nc.scalar.activation(out=g1[:], in_=g1ps[:, 0:E1], func=ACT.Copy)
-        for f in range(E2):
-            nc.scalar.copy(
-                out=w2w[f][:].bitcast(U16).rearrange("p (t m) -> p t m", t=4),
-                in_=w2raw[:, f, :].bitcast(U16).rearrange("p (m t) -> p t m", t=4),
-            )
 
         cpair = [keep.tile([P, T], F32, name=f"cpair{u}") for u in range(2)]
-        for e in range(E1):
+
+        def hidden(e):
             h, j = divmod(e, EH)
-            cols = slice(j * C1, (j + 1) * C1)
-            acc = psum.tile([P, H], F32, name="acc", tag="first", bufs=2)
+            if e == 0:
+                acc = psum.tile([P, H], F32, name="acc_first", tag="second", bufs=5)
+            else:
+                acc = psum.tile([P, H], F32, name="acc", tag="first", bufs=1)
             for s in range(PASSES):
+                words, scale_rows = tokens(e, s)
                 nc.tensor.matmul_mx(
                     out=acc[:],
-                    lhsT=xg[h][s][:, cols].bitcast(FP8X4),
-                    lhsT_scale=xsg[h][4 * s : P, cols],
+                    lhsT=words.bitcast(FP8X4),
+                    lhsT_scale=scale_rows,
                     rhs=w1w[e][:, s, :].bitcast(FP8X4),
                     rhs_scale=w1s[h][4 * h : P, j * PASSES + s, :],
                     start=(s == 0),
@@ -144,8 +163,11 @@ def tile_moe_ser_relu2_kernel(
                 in_=acc[:].rearrange("m (p u j) -> m u p j", u=2, j=2),
                 func=ACT.Relu,
             )
-            hb = ring.tile([P, H], BF16, name="hb")
-            if e not in VECTOR_GATED:
+            if e < E1 - 1:
+                hb = ring.tile([P, H], BF16, name="hb")
+            else:
+                hb = keep.tile([P, H], BF16, name="hb_last", tag="late", align_bytes=64)
+            if e < SCALAR_GATED:
                 r2 = ring.tile([P, H], F32, name="r2")
                 nc.scalar.activation(out=r2[:], in_=r[:], func=ACT.Square)
                 nc.scalar.activation(out=hb[:], in_=r2[:], func=ACT.Copy, scale=g1[:, e : e + 1])
@@ -153,6 +175,9 @@ def tile_moe_ser_relu2_kernel(
                 nc.vector.scalar_tensor_tensor(
                     out=hb[:], in0=r[:], scalar=g1[:, e : e + 1], in1=r[:], op0=MULT, op1=MULT
                 )
+            return hb
+
+        def put_back(e, hb):
             turned = psum.tile([P, 2, P], F32, name="turned", tag="turn", bufs=2)
             pairs = hb[:].bitcast(F32)
             for u in range(2):
@@ -163,7 +188,17 @@ def tile_moe_ser_relu2_kernel(
             for u in range(2):
                 nc.vector.tensor_copy(cpair[u][:].indirect(part), ct[:, u, :])
 
-        gated = {}
+        for e in range(E1):
+            put_back(e, hidden(e))
+
+        w2w = keep.tile([P, E2, 2 * N], U8, name="w2w", tag="late", align_bytes=64)
+        for f in range(E2):
+            nc.scalar.copy(
+                out=w2w[:, f, :].bitcast(U16).rearrange("p (t m) -> p t m", t=4),
+                in_=w2raw[:, f, :].bitcast(U16).rearrange("p (m t) -> p t m", t=4),
+            )
+
+        gated = [keep.tile([P, 2, T], F32, name=f"gated{a}") for a in range(2)]
         for f in range(E2):
             part = list2[:, f * C2 // 16 : (f + 1) * C2 // 16]
             gp = ring.tile([P, 2, C2], U32, name="gp")
@@ -177,61 +212,65 @@ def tile_moe_ser_relu2_kernel(
             cs = ring.tile([P, C2], U8, name="cs", align_bytes=64)
             nc.vector.quantize_mx(out=cq[:].bitcast(FP8X4), scales=cs[:], in_=cb[:])
             for a in range(2):
-                acc = psum.tile([P, N], F32, name="acc2", tag="second", bufs=4)
+                acc = psum.tile([P, N], F32, name="acc2", tag="second", bufs=5)
                 for j in range(2):
                     t = 2 * a + j
                     nc.tensor.matmul_mx(
                         out=acc[:, j * C2 : (j + 1) * C2],
-                        lhsT=w2w[f][:, 2 * t * P : 2 * (t + 1) * P].bitcast(FP4X4),
+                        lhsT=w2w[:, f, 2 * t * P : 2 * (t + 1) * P].bitcast(FP4X4),
                         lhsT_scale=w2s[:, f, t * P : (t + 1) * P],
                         rhs=cq[:].bitcast(FP8X4),
                         rhs_scale=cs[:],
                         start=True,
                         stop=True,
                     )
-                yg = keep.tile([P, 2, C2], F32, name=f"yg{f}_{a}")
                 nc.vector.tensor_tensor(
-                    out=yg[:],
+                    out=gated[a][:, :, f * C2 : (f + 1) * C2],
                     in0=acc[:].rearrange("p (j m) -> p j m", j=2),
                     in1=g2[:, f * C2 : (f + 1) * C2].unsqueeze(1).to_broadcast([P, 2, C2]),
                     op=MULT,
                 )
-                for j in range(2):
-                    gated[(f, 2 * a + j)] = yg[:, j, :]
 
-        tags = ("plane0", "w2w2", "plane2", "g2")
-        plane = [keep.tile([P, T], F32, name=f"plane{t}", tag=tags[t], align_bytes=64) for t in range(4)]
+        tags = ("plane0", "late", "plane2", "g2")
+        widths = (T, T, T, WIDE)
+        plane = [keep.tile([P, widths[t]], F32, name=f"plane{t}", tag=tags[t], align_bytes=64) for t in range(4)]
 
-        def scatter(f, t, on_scalar):
-            window = plane[t][:].indirect(list2[:, f * C2 // 16 : (f + 1) * C2 // 16])
+        def scatter(t, first, last, on_scalar):
+            target = plane[t][:].indirect(list2[:, first // 16 : last // 16])
+            values = gated[t // 2][:, t % 2, first:last]
             if on_scalar:
-                nc.scalar.activation(out=window, in_=gated[(f, t)], func=ACT.Copy)
+                nc.scalar.activation(out=target, in_=values, func=ACT.Copy)
             else:
-                nc.vector.tensor_copy(window, gated[(f, t)])
+                nc.vector.tensor_copy(target, values)
 
         rows = out_0.rearrange("(p t) n -> p t n", t=4)
         comb = keep.tile([P, 4, T], F32, name="comb")
-        for f, t in ((0, 0), (0, 2), (1, 0), (2, 0), (0, 1), (1, 1), (2, 1)):
-            scatter(f, t, True)
-        for f, t in ((1, 2), (2, 2), (0, 3), (1, 3), (2, 3)):
-            scatter(f, t, False)
+        scatter(0, 0, C2, True)
+        scatter(2, 0, C2, True)
+        scatter(0, C2, 2 * C2, True)
+        scatter(0, 2 * C2, T, True)
+        scatter(1, 0, T // 2, True)
+        scatter(1, T // 2, T, True)
+        scatter(2, C2, T, False)
+        scatter(3, 0, T, False)
         for t in (2, 0):
             nc.sync.dma_start(out=comb[:, t, :], in_=plane[t][:])
+        for t in (2, 0):
             nc.sync.dma_start(out=rows[:, t, :], in_=plane[t][:])
         nc.scalar.dma_start(out=rows[:, 1, :], in_=plane[1][:])
-        nc.sync.dma_start(out=rows[:, 3, :], in_=plane[3][:])
-        nc.vector.tensor_copy(out=comb[:, 3, :], in_=plane[3][:])
-        nc.vector.tensor_copy(out=comb[:, 1, :SPLIT], in_=plane[1][:, :SPLIT])
-        nc.scalar.copy(out=comb[:, 1, SPLIT:], in_=plane[1][:, SPLIT:])
+        nc.sync.dma_start(out=rows[:, 3, :], in_=plane[3][:, :T])
+        nc.scalar.copy(out=comb[:, 1, :], in_=plane[1][:])
+        nc.vector.tensor_copy(out=comb[:, 3, :], in_=plane[3][:, :T])
 
         codes = keep.tile([P, T], I32, name="codes", align_bytes=64)
         scales = keep.tile([P, T], U8, name="scales", align_bytes=64)
         words_out = out_1[0].rearrange("p t d -> p (t d)").bitcast(I32)
-        for cols in (slice(0, SPLIT), slice(SPLIT, T)):
-            ob = keep.tile([P, 4 * (cols.stop - cols.start)], BF16, name=f"ob{cols.start}", align_bytes=64)
+        for c in range(T // TOK):
+            cols = slice(c * TOK, (c + 1) * TOK)
+            ob = ring.tile([P, 4 * TOK], BF16, name="ob", align_bytes=64)
             dst = ob[:].rearrange("p (c i t) -> p c t i", i=4, t=4)
             src = comb[:, :, cols].rearrange("p t (c i) -> p c t i", i=4)
-            if cols.start:
+            if c == T // TOK - 1:
                 nc.scalar.copy(out=dst, in_=src)
             else:
                 nc.vector.tensor_copy(out=dst, in_=src)

from contextlib import ExitStack

import concourse.mybir as mybir
from concourse.masks import make_identity

K, T, E1, C1, E2, C2, H, N = 1536, 768, 6, 128, 3, 256, 512, 512
FLOPS = 2 * T * (K * H + H * N)

F32 = mybir.dt.float32
BF16 = mybir.dt.bfloat16
I32 = mybir.dt.int32
U32 = mybir.dt.uint32
U16 = mybir.dt.uint16
U8 = mybir.dt.uint8
FP8X4 = mybir.dt.float8_e4m3fn_x4
FP4X4 = mybir.dt.float4_e2m1fn_x4
ACT = mybir.ActivationFunctionType
MULT = mybir.AluOpType.mult

P = 128
PASSES = K // 512
EARLY = 3
SCALAR_GATED = 4
WIDE = 1024
EH = E1 // 2
TOK = 256


def tile_moe_ser_relu2_kernel(
    tc, x_words, x_scales, w1_words, w1_scales, w2_words, w2_scales, gate1, gate2, offs, offs2, out_0, out_1, out_2
):
    nc = tc.nc
    with ExitStack() as ctx:
        keep = ctx.enter_context(tc.tile_pool(name="keep", bufs=1))
        ring = ctx.enter_context(tc.tile_pool(name="ring", bufs=3))
        psum = ctx.enter_context(tc.psum_pool(name="psum", bufs=1))

        list1 = keep.tile([P, T // 16], U16, name="list1")
        list2 = keep.tile([P, T // 16], U16, name="list2")
        xw = keep.tile([P, PASSES * T], I32, name="xw", align_bytes=64)
        xs = keep.tile([P, T], U8, name="xs", tag="xs", align_bytes=64)
        xs_late = keep.tile([P, T], U8, name="xs_late", tag="xs_late", align_bytes=64)
        w1w = [keep.tile([P, PASSES, H], I32, name=f"w1w{e}", align_bytes=64) for e in range(E1)]
        w1s = [keep.tile([P, EH * PASSES, H], U8, name=f"w1s{h}", align_bytes=64) for h in range(2)]
        w2raw = keep.tile([P, E2, 2 * N], U8, name="w2raw", align_bytes=64)
        w2sraw = keep.tile([P, N], U8, name="w2sraw", align_bytes=64)
        w2s = keep.tile([P, E2, N], U8, name="w2s", align_bytes=64)
        g1rows = keep.tile([P, P], F32, name="g1rows")
        g1 = keep.tile([P, E1], F32, name="g1")
        g2 = keep.tile([P, T], F32, name="g2", tag="g2", align_bytes=64)
        ident = keep.tile([P, P], F32, name="ident")

        nc.gpsimd.memset(xs[:].bitcast(I32), 0)
        nc.gpsimd.memset(g1rows[:], 0.0)
        nc.gpsimd.memset(w2sraw[:].bitcast(I32), 0)
        make_identity(nc, ident[:])

        def load_x(first, last):
            nc.sync.dma_start(
                out=xw[:, first * T : last * T].rearrange("p (s t) -> p s t", t=T),
                in_=x_words[first:last].rearrange("s p t d -> p s (t d)").bitcast(I32),
            )

        def load_w1(e):
            nc.sync.dma_start(out=w1w[e][:], in_=w1_words[e].rearrange("s p i d -> p s (i d)").bitcast(I32))

        def load_w1_scales(h, r):
            rows = w1_scales.rearrange("e s b i -> b (e s) i")
            nc.sync.dma_start(
                out=w1s[h][4 * h + r : P : 32, :, :].bitcast(I32),
                in_=rows[r:16:4, EH * PASSES * h : EH * PASSES * (h + 1), :].bitcast(I32),
            )

        nc.sync.dma_start(list1[:], offs)
        load_x(0, 1)
        for r in range(3):
            load_w1_scales(0, r)
        load_x(1, PASSES)
        load_w1(0)
        load_w1_scales(0, 3)
        for q in range(4):
            nc.sync.dma_start(
                out=xs[32 * q : 32 * q + 4 * PASSES, :].bitcast(I32), in_=x_scales[:, 4 * q : 4 * q + 4, :].bitcast(I32)
            )
        nc.sync.dma_start(out=g1rows[0:E1, :], in_=gate1[0:1, :].rearrange("o (e p) -> (o e) p", p=P))
        load_w1(1)
        nc.sync.dma_start(out=w2raw[:].bitcast(I32), in_=w2_words.rearrange("f s p b -> p (f s) b").bitcast(I32))
        nc.sync.dma_start(
            out=w2sraw[0 : 16 * E2, :].bitcast(I32), in_=w2_scales.rearrange("f s b n -> b (f s) n").bitcast(I32)
        )
        load_w1(2)
        for r in range(4):
            load_w1_scales(1, r)
        for e in range(EH, E1):
            load_w1(e)
        nc.sync.dma_start(list2[:], offs2)
        nc.sync.dma_start(out=g2[:], in_=gate2)

        cut = EARLY * C1
        early, late = list1[:, : cut // 16], list1[:, cut // 16 :]
        xg_early = keep.tile([P, PASSES, cut], U32, name="xg_early", align_bytes=64)
        xg_first = keep.tile([P, T - cut], U32, name="xg_first", align_bytes=64)
        xsg_early = keep.tile([P, cut], U8, name="xsg_early", align_bytes=64)
        xsg_late = keep.tile([P, T - cut], U8, name="xsg_late", align_bytes=64)

        def window(s):
            return xw[:, s * T : (s + 1) * T].bitcast(U32)

        for s in range(PASSES):
            nc.vector.tensor_copy(xg_early[:, s, :], window(s).indirect(early))
        nc.vector.tensor_copy(xsg_early[:], xs[:].indirect(early))
        nc.vector.tensor_copy(xg_first[:], window(0).indirect(late))
        nc.vector.tensor_copy(out=xs_late[:].bitcast(I32), in_=xs[:].bitcast(I32))
        xg_rest = keep.tile([P, PASSES - 1, T - cut], U32, name="xg_rest", tag="xs", align_bytes=64)
        for s in range(1, PASSES):
            nc.vector.tensor_copy(xg_rest[:, s - 1, :], window(s).indirect(late))
        nc.vector.tensor_copy(xsg_late[:], xs_late[:].indirect(late))

        def tokens(e, s):
            if e < EARLY:
                cols = slice(e * C1, (e + 1) * C1)
                return xg_early[:, s, cols], xsg_early[4 * s : P, cols]
            cols = slice((e - EARLY) * C1, (e - EARLY + 1) * C1)
            words = xg_first[:, cols] if s == 0 else xg_rest[:, s - 1, cols]
            return words, xsg_late[4 * s : P, cols]

        w2sdealt = keep.tile([P, N], U8, name="w2sdealt", tag="xs_late", align_bytes=64)
        nc.vector.tensor_copy(
            out=w2sdealt[:].rearrange("p (t m) -> p t m", t=4), in_=w2sraw[:].rearrange("p (m t) -> p t m", t=4)
        )
        for q in range(4):
            nc.gpsimd.dma_start(
                out=w2s[32 * q : 32 * q + 4, :, :].bitcast(I32),
                in_=w2sdealt[4 * E2 * q : 4 * E2 * (q + 1), :].bitcast(I32),
            )

        g1ps = psum.tile([P, N], F32, name="g1ps", tag="second", bufs=5)
        nc.tensor.transpose(g1ps[:, 0:P], g1rows[:], ident[:])
        nc.scalar.activation(out=g1[:], in_=g1ps[:, 0:E1], func=ACT.Copy)

        cpair = [keep.tile([P, T], F32, name=f"cpair{u}") for u in range(2)]

        def hidden(e):
            h, j = divmod(e, EH)
            if e == 0:
                acc = psum.tile([P, H], F32, name="acc_first", tag="second", bufs=5)
            else:
                acc = psum.tile([P, H], F32, name="acc", tag="first", bufs=1)
            for s in range(PASSES):
                words, scale_rows = tokens(e, s)
                nc.tensor.matmul_mx(
                    out=acc[:],
                    lhsT=words.bitcast(FP8X4),
                    lhsT_scale=scale_rows,
                    rhs=w1w[e][:, s, :].bitcast(FP8X4),
                    rhs_scale=w1s[h][4 * h : P, j * PASSES + s, :],
                    start=(s == 0),
                    stop=(s == PASSES - 1),
                )
            r = ring.tile([P, H], F32, name="r")
            nc.scalar.activation(
                out=r[:].rearrange("m (u p j) -> m u p j", u=2, j=2),
                in_=acc[:].rearrange("m (p u j) -> m u p j", u=2, j=2),
                func=ACT.Relu,
            )
            if e < E1 - 1:
                hb = ring.tile([P, H], BF16, name="hb")
            else:
                hb = keep.tile([P, H], BF16, name="hb_last", tag="late", align_bytes=64)
            if e < SCALAR_GATED:
                r2 = ring.tile([P, H], F32, name="r2")
                nc.scalar.activation(out=r2[:], in_=r[:], func=ACT.Square)
                nc.scalar.activation(out=hb[:], in_=r2[:], func=ACT.Copy, scale=g1[:, e : e + 1])
            else:
                nc.vector.scalar_tensor_tensor(
                    out=hb[:], in0=r[:], scalar=g1[:, e : e + 1], in1=r[:], op0=MULT, op1=MULT
                )
            return hb

        def put_back(e, hb):
            turned = psum.tile([P, 2, P], F32, name="turned", tag="turn", bufs=2)
            pairs = hb[:].bitcast(F32)
            for u in range(2):
                nc.tensor.transpose(turned[:, u, :], pairs[:, u * P : (u + 1) * P], ident[:])
            ct = ring.tile([P, 2, P], F32, name="ct")
            nc.scalar.copy(out=ct[:], in_=turned[:])
            part = list1[:, e * C1 // 16 : (e + 1) * C1 // 16]
            for u in range(2):
                nc.vector.tensor_copy(cpair[u][:].indirect(part), ct[:, u, :])

        for e in range(E1):
            put_back(e, hidden(e))

        w2w = keep.tile([P, E2, 2 * N], U8, name="w2w", tag="late", align_bytes=64)
        for f in range(E2):
            nc.scalar.copy(
                out=w2w[:, f, :].bitcast(U16).rearrange("p (t m) -> p t m", t=4),
                in_=w2raw[:, f, :].bitcast(U16).rearrange("p (m t) -> p t m", t=4),
            )

        gated = [keep.tile([P, 2, T], F32, name=f"gated{a}") for a in range(2)]
        for f in range(E2):
            part = list2[:, f * C2 // 16 : (f + 1) * C2 // 16]
            gp = ring.tile([P, 2, C2], U32, name="gp")
            for u in range(2):
                nc.vector.tensor_copy(gp[:, u, :], cpair[u][:].bitcast(U32).indirect(part))
            cb = ring.tile([P, 4 * C2], BF16, name="cb", align_bytes=64)
            nc.scalar.copy(
                out=cb[:].bitcast(U32).rearrange("p (m u) -> p m u", u=2), in_=gp[:].rearrange("p u m -> p m u")
            )
            cq = ring.tile([P, C2], U32, name="cq", align_bytes=64)
            cs = ring.tile([P, C2], U8, name="cs", align_bytes=64)
            nc.vector.quantize_mx(out=cq[:].bitcast(FP8X4), scales=cs[:], in_=cb[:])
            for a in range(2):
                acc = psum.tile([P, N], F32, name="acc2", tag="second", bufs=5)
                for j in range(2):
                    t = 2 * a + j
                    nc.tensor.matmul_mx(
                        out=acc[:, j * C2 : (j + 1) * C2],
                        lhsT=w2w[:, f, 2 * t * P : 2 * (t + 1) * P].bitcast(FP4X4),
                        lhsT_scale=w2s[:, f, t * P : (t + 1) * P],
                        rhs=cq[:].bitcast(FP8X4),
                        rhs_scale=cs[:],
                        start=True,
                        stop=True,
                    )
                nc.vector.tensor_tensor(
                    out=gated[a][:, :, f * C2 : (f + 1) * C2],
                    in0=acc[:].rearrange("p (j m) -> p j m", j=2),
                    in1=g2[:, f * C2 : (f + 1) * C2].unsqueeze(1).to_broadcast([P, 2, C2]),
                    op=MULT,
                )

        tags = ("plane0", "late", "plane2", "g2")
        widths = (T, T, T, WIDE)
        plane = [keep.tile([P, widths[t]], F32, name=f"plane{t}", tag=tags[t], align_bytes=64) for t in range(4)]

        def scatter(t, first, last, on_scalar):
            target = plane[t][:].indirect(list2[:, first // 16 : last // 16])
            values = gated[t // 2][:, t % 2, first:last]
            if on_scalar:
                nc.scalar.activation(out=target, in_=values, func=ACT.Copy)
            else:
                nc.vector.tensor_copy(target, values)

        rows = out_0.rearrange("(p t) n -> p t n", t=4)
        comb = keep.tile([P, 4, T], F32, name="comb")
        scatter(0, 0, C2, True)
        scatter(2, 0, C2, True)
        scatter(0, C2, 2 * C2, True)
        scatter(0, 2 * C2, T, True)
        scatter(1, 0, T // 2, True)
        scatter(1, T // 2, T, True)
        scatter(2, C2, T, False)
        scatter(3, 0, T, False)
        for t in (2, 0):
            nc.sync.dma_start(out=comb[:, t, :], in_=plane[t][:])
        for t in (2, 0):
            nc.sync.dma_start(out=rows[:, t, :], in_=plane[t][:])
        nc.scalar.dma_start(out=rows[:, 1, :], in_=plane[1][:])
        nc.sync.dma_start(out=rows[:, 3, :], in_=plane[3][:, :T])
        nc.scalar.copy(out=comb[:, 1, :], in_=plane[1][:])
        nc.vector.tensor_copy(out=comb[:, 3, :], in_=plane[3][:, :T])

        codes = keep.tile([P, T], I32, name="codes", align_bytes=64)
        scales = keep.tile([P, T], U8, name="scales", align_bytes=64)
        words_out = out_1[0].rearrange("p t d -> p (t d)").bitcast(I32)
        for c in range(T // TOK):
            cols = slice(c * TOK, (c + 1) * TOK)
            ob = ring.tile([P, 4 * TOK], BF16, name="ob", align_bytes=64)
            dst = ob[:].rearrange("p (c i t) -> p c t i", i=4, t=4)
            src = comb[:, :, cols].rearrange("p t (c i) -> p c t i", i=4)
            if c == T // TOK - 1:
                nc.scalar.copy(out=dst, in_=src)
            else:
                nc.vector.tensor_copy(out=dst, in_=src)
            nc.vector.quantize_mx(out=codes[:, cols].bitcast(FP8X4), scales=scales[:, cols], in_=ob[:])
            nc.sync.dma_start(out=words_out[:, cols], in_=codes[:, cols])
        for q in range(4):
            queue = nc.scalar if q % 2 else nc.sync
            queue.dma_start(
                out=out_2[0, 4 * q : 4 * q + 4, :].bitcast(I32), in_=scales[32 * q : 32 * q + 4, :].bitcast(I32)
            )
